import numpy as np
import ml_dtypes


def mxq(x, axis, fmt="e4m3"):
    dtype, down = {"e4m3": (ml_dtypes.float8_e4m3fn, 7), "e5m2": (ml_dtypes.float8_e5m2, 14)}[fmt]
    v = np.moveaxis(np.asarray(x, np.float32).astype(ml_dtypes.bfloat16).astype(np.float64), axis, -1)
    blocks = v.reshape(v.shape[:-1] + (-1, 32))
    amax = np.abs(blocks).max(-1, keepdims=True)
    byte = np.maximum(np.where(amax > 0, np.frexp(amax)[1] - 1 + 127, 0) - down, 1)
    scale = np.exp2(byte - 127.0)
    codes = (blocks / scale).astype(np.float32).astype(dtype).astype(np.float64)
    return np.moveaxis((codes * scale).reshape(v.shape), -1, axis)


WIDE = False


def mx_kscale(k):
    if not WIDE:
        return np.ones(k)
    levels = np.array([10, -10, 5, -5, 0])
    if k % 512:
        return np.exp2(np.random.permutation(np.resize(levels, k // 32))).repeat(32)
    a = np.empty((k // 512, 16))
    for p in range(k // 512):
        a[p, :8] = np.random.permutation(np.resize(levels, 8))
        for g in range(8):
            far = levels[np.abs(levels - a[p, g]) >= 10]
            a[p, g + 8] = far[np.random.randint(len(far))]
    return np.exp2(a.ravel()).repeat(32)


def f64(x):
    return np.asarray(x).astype(np.float64)


def striped8(idx):
    return np.asarray(idx).reshape(8, -1, 16).transpose(0, 2, 1).reshape(128, -1).astype(np.uint16)


def unstriped8(offs):
    return offs.reshape(8, 16, -1).transpose(0, 2, 1).reshape(8, -1).astype(np.int64)


def pick8(x, idx, run):
    r = np.arange(len(x))
    return x[r[:, None], idx[r % (8 * run) // run]]


E2M1 = np.array([0.0, 0.5, 1.0, 1.5, 2.0, 3.0, 4.0, 6.0, -0.0, -0.5, -1.0, -1.5, -2.0, -3.0, -4.0, -6.0])


def pack_weight(w, fmt):
    k, n = w.shape
    w = f64(np.asarray(w, np.float32).astype(ml_dtypes.bfloat16)).reshape(k // 32, 32, n)
    amax = np.abs(w).max(1)
    if fmt == "e4m3":
        byte = np.frexp(amax)[1] - 1 + 127 - 7
    else:
        mant, ex = np.frexp(amax / 6.0)
        byte = np.where(mant > 0.5, ex, ex - 1) + 127
    byte = np.clip(np.where(amax > 0, byte, 1), 1, 254)
    scaled = (w * np.exp2(127.0 - byte)[:, None, :]).reshape(k, n).astype(np.float32)
    by_word = np.ascontiguousarray(scaled.reshape(k // 512, 128, 4, n).transpose(0, 1, 3, 2))
    if fmt == "e4m3":
        words = by_word.astype(ml_dtypes.float8_e4m3fn).view(np.uint8)
    else:
        c = by_word.astype(ml_dtypes.float4_e2m1fn).view(np.uint8) & 0xF
        words = (c[..., 0::2] | (c[..., 1::2] << 4)).reshape(k // 512, 128, 2 * n)
    return np.ascontiguousarray(words), np.ascontiguousarray(byte.astype(np.uint8).reshape(k // 512, 16, n))


def unpack_weight(words, scales, fmt):
    g, _, n = scales.shape
    words = np.ascontiguousarray(words).reshape(g, 128, n, -1)
    if fmt == "e4m3":
        vals = words.view(ml_dtypes.float8_e4m3fn).astype(np.float64)
    else:
        nib = np.empty((g, 128, n, 4), np.uint8)
        nib[..., 0::2] = words & 0xF
        nib[..., 1::2] = words >> 4
        vals = E2M1[nib]
    vals = vals * np.repeat(np.exp2(scales.astype(np.float64) - 127.0), 8, axis=1)[..., None]
    return vals.transpose(0, 1, 3, 2).reshape(g * 512, n)


D, V, Q, I = 512, 2048, 128, 512


def setup_inputs():
    n = np.random.standard_normal
    idx = np.stack([np.random.permutation(V)[:I] for _ in range(8)])
    fd = mx_kscale(D)
    vocp = pack_weight(n((D, V)) / fd[:, None], "e4m3")
    return {
        "hid": (n((D, Q)) * 1.0 / np.sqrt(D) * fd[:, None]).astype(np.float32),
        "voc_words": vocp[0],
        "voc_scales": vocp[1],
        "mult": (np.random.uniform(100.0, 300.0, (Q, 1))).astype(np.float32),
        "sw": (np.random.uniform(0.005, 0.02, (1, I))).astype(np.float32),
        "old": (0.5 * n((Q, V))).astype(np.float32),
        "offs": striped8(idx),
    }


def reference(hid, voc_words, voc_scales, mult, sw, old, offs):
    idx = unstriped8(offs)
    vocu = unpack_weight(voc_words, voc_scales, "e4m3")
    hidq = mxq(f64(hid), 0, "e4m3")
    a = hidq.T @ vocu
    m1 = np.max(a, axis=1, keepdims=True)
    p = np.exp(a - m1)
    z = np.sum(p, axis=1, keepdims=True)
    px = np.exp(pick8(a, idx, 16) - m1)
    u1 = px / z
    du1 = f64(sw) * (1.0 - u1 * f64(mult)) / u1 + f64(sw) * np.log(u1) * (-1.0) * f64(mult)
    dpx = du1 / z
    dz = np.sum(du1 * px / np.square(z) * (-1.0), axis=1, keepdims=True)
    e1 = dpx * px
    s1 = np.zeros((Q, V))
    s1[np.arange(Q)[:, None], idx[np.arange(Q) % 128 // 16]] = e1
    da = dz * p + s1
    y = da * 64.0 + f64(old)
    return y

@@ -1,0 +1,190 @@
+import math
+from contextlib import ExitStack
+
+import concourse.mybir as mybir
+from concourse.masks import make_identity
+
+D, V, Q, I = 512, 2048, 128, 512
+FLOPS = 2 * D * Q * V
+
+F32 = mybir.dt.float32
+BF16 = mybir.dt.bfloat16
+I32 = mybir.dt.int32
+U32 = mybir.dt.uint32
+U16 = mybir.dt.uint16
+U8 = mybir.dt.uint8
+FP8X4 = mybir.dt.float8_e4m3fn_x4
+ALU = mybir.AluOpType
+ACT = mybir.ActivationFunctionType
+AXIS = mybir.AxisListType
+
+P = 128
+PACK = 4
+BLOCK = 512
+CHUNKS = [(0, 256), (256, 256), (512, 512), (1024, 512), (1536, 512)]
+PAD = 8
+LOAD = 1024
+
+NODE_STEP = 0.375
+NODE_HI, NODE_LO = 9, -86
+NODES = NODE_HI - NODE_LO + 1
+NODE_CONST = NODE_STEP * sum(math.exp(-math.exp(NODE_STEP * j)) for j in range(NODE_LO, NODE_HI + 1))
+
+
+def tile_attend_bfocal_heads_kernel(tc, hid, voc_words, voc_scales, mult, sw, old, offs, out):
+    nc = tc.nc
+    n = len(CHUNKS)
+    with ExitStack() as ctx:
+        sb = ctx.enter_context(tc.tile_pool(name="sb", bufs=1))
+        ps = ctx.enter_context(tc.psum_pool(name="ps", bufs=1))
+
+        planes = sb.tile([P, BLOCK], U8, align_bytes=64)
+        nc.gpsimd.memset(planes[:].bitcast(I32), 0)
+
+        hid_raw = sb.tile([P, PACK, Q], F32, tag="stage")
+        nc.sync.dma_start(out=hid_raw[:], in_=hid.rearrange("(p t) q -> p t q", t=PACK))
+        sw_cols = sb.tile([P, PACK], F32)
+        nc.sync.dma_start(out=sw_cols[:], in_=sw.rearrange("o (p t) -> (o p) t", t=PACK))
+        for quad in range(4):
+            rows = voc_scales[0, 4 * quad : 4 * quad + 4, :].bitcast(I32)
+            nc.sync.dma_start(
+                out=planes[32 * quad : 32 * quad + 16, :].bitcast(I32),
+                in_=rows.rearrange("r (b c) -> b r c", b=V // BLOCK),
+            )
+        words = []
+        voc_bytes = voc_words[0].rearrange("p n t -> p (n t)")
+        for b in range(V // LOAD):
+            w = sb.tile([P, LOAD], U32, align_bytes=64, name=f"words{b}")
+            nc.sync.dma_start(
+                out=w[:].bitcast(I32),
+                in_=voc_bytes[:, PACK * LOAD * b : PACK * LOAD * (b + 1)].bitcast(I32),
+            )
+            words.append(w)
+        offsets = sb.tile([P, I // 16], U16)
+        nc.sync.dma_start(offsets[:], offs)
+
+        placed = sb.tile([P, V], F32)
+        nc.vector.memset(placed[:], 0.0)
+
+        steps = sb.tile([P, NODES], F32)
+        nc.gpsimd.iota(steps[:], pattern=[[-1, NODES]], base=NODE_HI, channel_multiplier=0,
+                       allow_small_or_imprecise_dtypes=True)
+        nodes = sb.tile([P, NODES], F32)
+        nc.scalar.activation(nodes[:], steps[:], ACT.Exp, scale=NODE_STEP)
+        ident = sb.tile([P, P], F32)
+        make_identity(nc, ident[:])
+        mult_col = sb.tile([P, 1], F32)
+        nc.gpsimd.dma_start(out=mult_col[:], in_=mult)
+
+        hid_bf = sb.tile([P, Q, PACK], BF16, align_bytes=64)
+        hid_codes = sb.tile([P, Q], U32, align_bytes=64)
+        hid_scales = sb.tile([P, Q], U8, align_bytes=64)
+        half = Q // 2
+        for u in range(2):
+            qs = slice(u * half, (u + 1) * half)
+            nc.vector.tensor_copy(
+                out=hid_bf[:, qs, :].rearrange("p (c i) t -> p c t i", i=4),
+                in_=hid_raw[:, :, qs].rearrange("p t (c i) -> p c t i", i=4),
+            )
+        old_sb = sb.tile([P, V], F32, tag="stage")
+        nc.sync.dma_start(out=old_sb[:], in_=old)
+        for u in range(2):
+            qs = slice(u * half, (u + 1) * half)
+            nc.vector.quantize_mx(
+                out=hid_codes[:, qs].bitcast(FP8X4),
+                scales=hid_scales[:, qs],
+                in_=hid_bf[:, qs, :].rearrange("p q t -> p (q t)"),
+            )
+
+        sw_bank = ps.tile([P, PACK, P], F32)
+        for t in range(PACK):
+            nc.tensor.transpose(sw_bank[:, t, :], sw_cols[:, t : t + 1].to_broadcast([P, P]), ident[:])
+        sw64 = sb.tile([P, I], F32)
+        sw_sum = sb.tile([P, 1], F32)
+        nc.scalar.activation(
+            sw64[:].rearrange("p (s t) -> p s t", t=PACK),
+            sw_bank[:].rearrange("p t s -> p s t"),
+            ACT.Identity, scale=64.0, accum_out=sw_sum[:],
+        )
+
+        sw_half_sum = sb.tile([P, 1], F32)
+        nc.gpsimd.tensor_scalar(sw_half_sum[:], sw_sum[:], 0.5, 0.0, ALU.mult, ALU.add)
+        scores = sb.tile([P, V], F32)
+        probs = sb.tile([P, V], F32)
+        chunk_max = sb.tile([P, n], F32)
+        chunk_sum = sb.tile([P, n], F32)
+        neg_ref = sb.tile([P, n, PAD], F32)
+        neg_max = neg_ref[:, n - 1, 0:1]
+        rescale = sb.tile([P, n], F32)
+        shift = sb.tile([P, 1], F32)
+        for c, (c0, width) in enumerate(CHUNKS):
+            b, off = divmod(c0, BLOCK)
+            bank = ps.tile([P, width], F32, name=f"bank{c}")
+            nc.tensor.matmul_mx(
+                out=bank[:],
+                lhsT=hid_codes[:].bitcast(FP8X4),
+                lhsT_scale=hid_scales[:],
+                rhs=words[c0 // LOAD][:, c0 % LOAD : c0 % LOAD + width].bitcast(FP8X4),
+                rhs_scale=planes[4 * b : P, off : off + width],
+                start=True,
+                stop=True,
+            )
+            cols = slice(c0, c0 + width)
+            nc.vector.tensor_scalar(scores[:, cols], bank[:], 1.0, None, ALU.mult, ALU.max,
+                                    accum_out=chunk_max[:, c : c + 1])
+            if c < n - 1:
+                nc.gpsimd.tensor_scalar(neg_ref[:, c, 0:1], chunk_max[:, c : c + 1], -1.0, 0.0, ALU.mult, ALU.add)
+            else:
+                nc.vector.tensor_reduce(neg_max, chunk_max[:], AXIS.X, ALU.max, negate=True)
+                nc.scalar.activation(rescale[:], neg_ref[:, :, 0], ACT.Exp, scale=-1.0, bias=neg_max)
+                nc.scalar.activation(shift[:], neg_max, ACT.Identity, bias=1.0 - NODE_CONST)
+            nc.scalar.activation(probs[:, cols], scores[:, cols], ACT.Exp, bias=neg_ref[:, c, 0:1],
+                                 accum_out=chunk_sum[:, c : c + 1])
+
+        picked = sb.tile([P, I], F32)
+        nc.vector.tensor_copy(picked[:], scores[:].indirect(offsets[:]))
+
+        terms = sb.tile([P, n], F32)
+        neg_z = sb.tile([P, 1], F32)
+        nc.vector.scalar_tensor_tensor(terms[:], rescale[:], -1.0, chunk_sum[:], ALU.mult, ALU.mult,
+                                       accum_out=neg_z[:])
+        picked_p = sb.tile([P, I], F32)
+        nc.scalar.activation(picked_p[:], picked[:], ACT.Exp, bias=neg_max)
+        decay = sb.tile([P, NODES], F32)
+        decay_sum = sb.tile([P, 1], F32)
+        nc.scalar.activation(decay[:], nodes[:], ACT.Exp, scale=neg_z[:], accum_out=decay_sum[:])
+
+        log_part = sb.tile([P, I], F32)
+        nc.vector.tensor_scalar(log_part[:], picked[:], shift[:], 1.0 / NODE_STEP, ALU.add, ALU.mult)
+        neg_inv_z = sb.tile([P, 1], F32)
+        nc.vector.reciprocal(neg_inv_z[:], neg_z[:])
+        row_factor = sb.tile([P, 1], F32)
+        nc.vector.tensor_scalar(row_factor[:], neg_inv_z[:], mult_col[:], NODE_STEP, ALU.mult, ALU.mult)
+        weight = sb.tile([P, I], F32)
+        focal = sb.tile([P, I], F32)
+        focal_sum = sb.tile([P, 2], F32)
+        halves = [slice(0, I // 2), slice(I // 2, I)]
+        for s in halves:
+            nc.vector.scalar_tensor_tensor(weight[:, s], picked_p[:, s], row_factor[:], sw64[:, s], ALU.mult, ALU.mult)
+        for u, s in enumerate(halves):
+            nc.vector.scalar_tensor_tensor(focal[:, s], log_part[:, s], decay_sum[:], weight[:, s], ALU.add, ALU.mult,
+                                           accum_out=focal_sum[:, u : u + 1])
+        nc.vector.tensor_tensor(placed[:].indirect(offsets[:]), focal[:], sw64[:], ALU.add)
+
+        norm = sb.tile([P, n], F32)
+        nc.scalar.activation(norm[:], rescale[:], ACT.Identity, scale=neg_inv_z[:])
+        total_parts = sb.tile([P, 2], F32)
+        total = sb.tile([P, 1], F32)
+        nc.scalar.activation(total_parts[:], focal_sum[:], ACT.Identity, bias=sw_half_sum[:], accum_out=total[:])
+        coef = sb.tile([P, n], F32)
+        nc.scalar.activation(coef[:], norm[:], ACT.Identity, scale=total[:])
+
+        base = sb.tile([P, V], F32)
+        result = sb.tile([P, V], F32)
+        for c in reversed(range(n)):
+            c0, width = CHUNKS[c]
+            cols = slice(c0, c0 + width)
+            nc.vector.scalar_tensor_tensor(base[:, cols], probs[:, cols], coef[:, c : c + 1], old_sb[:, cols],
+                                           ALU.mult, ALU.add)
+            nc.vector.tensor_tensor(result[:, cols], base[:, cols], placed[:, cols], ALU.add)
+            nc.sync.dma_start(out=out[:, cols], in_=result[:, cols])

@@ -23,7 +23,9 @@ PACK = 4
 BLOCK = 512
 CHUNKS = [(0, 256), (256, 256), (512, 512), (1024, 512), (1536, 512)]
 PAD = 8
-LOAD = 1024
+PIECE = 256
+LEAD = 3
+LOAD = 512
 
 NODE_STEP = 0.375
 NODE_HI, NODE_LO = 9, -86
@@ -43,8 +45,6 @@ def tile_attend_bfocal_heads_kernel(tc, hid, voc_words, voc_scales, mult, sw, ol
 
         hid_raw = sb.tile([P, PACK, Q], F32, tag="stage")
         nc.sync.dma_start(out=hid_raw[:], in_=hid.rearrange("(p t) q -> p t q", t=PACK))
-        sw_cols = sb.tile([P, PACK], F32)
-        nc.sync.dma_start(out=sw_cols[:], in_=sw.rearrange("o (p t) -> (o p) t", t=PACK))
         for quad in range(4):
             rows = voc_scales[0, 4 * quad : 4 * quad + 4, :].bitcast(I32)
             nc.sync.dma_start(
@@ -60,21 +60,23 @@ def tile_attend_bfocal_heads_kernel(tc, hid, voc_words, voc_scales, mult, sw, ol
                 in_=voc_bytes[:, PACK * LOAD * b : PACK * LOAD * (b + 1)].bitcast(I32),
             )
             words.append(w)
+        sw_cols = sb.tile([P, PACK], F32)
+        nc.sync.dma_start(out=sw_cols[:], in_=sw.rearrange("o (p t) -> (o p) t", t=PACK))
+        mult_col = sb.tile([P, 1], F32)
+        nc.sync.dma_start(out=mult_col[:], in_=mult)
         offsets = sb.tile([P, I // 16], U16)
         nc.sync.dma_start(offsets[:], offs)
 
         placed = sb.tile([P, V], F32)
         nc.vector.memset(placed[:], 0.0)
 
+        ident = sb.tile([P, P], F32)
+        make_identity(nc, ident[:])
         steps = sb.tile([P, NODES], F32)
         nc.gpsimd.iota(steps[:], pattern=[[-1, NODES]], base=NODE_HI, channel_multiplier=0,
                        allow_small_or_imprecise_dtypes=True)
         nodes = sb.tile([P, NODES], F32)
         nc.scalar.activation(nodes[:], steps[:], ACT.Exp, scale=NODE_STEP)
-        ident = sb.tile([P, P], F32)
-        make_identity(nc, ident[:])
-        mult_col = sb.tile([P, 1], F32)
-        nc.gpsimd.dma_start(out=mult_col[:], in_=mult)
 
         hid_bf = sb.tile([P, Q, PACK], BF16, align_bytes=64)
         hid_codes = sb.tile([P, Q], U32, align_bytes=64)
@@ -96,19 +98,6 @@ def tile_attend_bfocal_heads_kernel(tc, hid, voc_words, voc_scales, mult, sw, ol
                 in_=hid_bf[:, qs, :].rearrange("p q t -> p (q t)"),
             )
 
-        sw_bank = ps.tile([P, PACK, P], F32)
-        for t in range(PACK):
-            nc.tensor.transpose(sw_bank[:, t, :], sw_cols[:, t : t + 1].to_broadcast([P, P]), ident[:])
-        sw64 = sb.tile([P, I], F32)
-        sw_sum = sb.tile([P, 1], F32)
-        nc.scalar.activation(
-            sw64[:].rearrange("p (s t) -> p s t", t=PACK),
-            sw_bank[:].rearrange("p t s -> p s t"),
-            ACT.Identity, scale=64.0, accum_out=sw_sum[:],
-        )
-
-        sw_half_sum = sb.tile([P, 1], F32)
-        nc.gpsimd.tensor_scalar(sw_half_sum[:], sw_sum[:], 0.5, 0.0, ALU.mult, ALU.add)
         scores = sb.tile([P, V], F32)
         probs = sb.tile([P, V], F32)
         chunk_max = sb.tile([P, n], F32)
@@ -119,7 +108,7 @@ def tile_attend_bfocal_heads_kernel(tc, hid, voc_words, voc_scales, mult, sw, ol
         shift = sb.tile([P, 1], F32)
         for c, (c0, width) in enumerate(CHUNKS):
             b, off = divmod(c0, BLOCK)
-            bank = ps.tile([P, width], F32, name=f"bank{c}")
+            bank = ps.tile([P, width], F32, name=f"score{c}", tag=f"bank{c}")
             nc.tensor.matmul_mx(
                 out=bank[:],
                 lhsT=hid_codes[:].bitcast(FP8X4),
@@ -141,6 +130,16 @@ def tile_attend_bfocal_heads_kernel(tc, hid, voc_words, voc_scales, mult, sw, ol
             nc.scalar.activation(probs[:, cols], scores[:, cols], ACT.Exp, bias=neg_ref[:, c, 0:1],
                                  accum_out=chunk_sum[:, c : c + 1])
 
+        sw_bank = ps.tile([P, PACK, P], F32, tag=f"bank{n - 1}")
+        for t in range(PACK):
+            nc.tensor.transpose(sw_bank[:, t, :], sw_cols[:, t : t + 1].to_broadcast([P, P]), ident[:])
+        row_scale = sb.tile([P, 1], F32)
+        nc.gpsimd.tensor_scalar(row_scale[:], mult_col[:], 64.0 * NODE_STEP, 0.0, ALU.mult, ALU.add)
+        sw_in_order = sw_bank[:].rearrange("p t s -> p s t")
+        sw_mult = sb.tile([P, I], F32)
+        nc.scalar.activation(sw_mult[:].rearrange("p (s t) -> p s t", t=PACK), sw_in_order, ACT.Copy,
+                             scale=row_scale[:])
+
         picked = sb.tile([P, I], F32)
         nc.vector.tensor_copy(picked[:], scores[:].indirect(offsets[:]))
 
@@ -148,24 +147,28 @@ def tile_attend_bfocal_heads_kernel(tc, hid, voc_words, voc_scales, mult, sw, ol
         neg_z = sb.tile([P, 1], F32)
         nc.vector.scalar_tensor_tensor(terms[:], rescale[:], -1.0, chunk_sum[:], ALU.mult, ALU.mult,
                                        accum_out=neg_z[:])
+        halves = [slice(0, I // 2), slice(I // 2, I)]
         picked_p = sb.tile([P, I], F32)
-        nc.scalar.activation(picked_p[:], picked[:], ACT.Exp, bias=neg_max)
-        decay = sb.tile([P, NODES], F32)
+        for s in halves:
+            nc.scalar.activation(picked_p[:, s], picked[:, s], ACT.Exp, bias=neg_max)
+        decay = sb.tile([P, NODES], F32, tag="stage2")
         decay_sum = sb.tile([P, 1], F32)
         nc.scalar.activation(decay[:], nodes[:], ACT.Exp, scale=neg_z[:], accum_out=decay_sum[:])
+        sw64 = sb.tile([P, I], F32, tag="stage2")
+        sw_sum = sb.tile([P, 1], F32)
+        nc.scalar.activation(sw64[:].rearrange("p (s t) -> p s t", t=PACK), sw_in_order, ACT.Identity,
+                             scale=64.0, accum_out=sw_sum[:])
 
         log_part = sb.tile([P, I], F32)
         nc.vector.tensor_scalar(log_part[:], picked[:], shift[:], 1.0 / NODE_STEP, ALU.add, ALU.mult)
         neg_inv_z = sb.tile([P, 1], F32)
         nc.vector.reciprocal(neg_inv_z[:], neg_z[:])
-        row_factor = sb.tile([P, 1], F32)
-        nc.vector.tensor_scalar(row_factor[:], neg_inv_z[:], mult_col[:], NODE_STEP, ALU.mult, ALU.mult)
         weight = sb.tile([P, I], F32)
         focal = sb.tile([P, I], F32)
         focal_sum = sb.tile([P, 2], F32)
-        halves = [slice(0, I // 2), slice(I // 2, I)]
         for s in halves:
-            nc.vector.scalar_tensor_tensor(weight[:, s], picked_p[:, s], row_factor[:], sw64[:, s], ALU.mult, ALU.mult)
+            nc.vector.scalar_tensor_tensor(weight[:, s], picked_p[:, s], neg_inv_z[:], sw_mult[:, s],
+                                           ALU.mult, ALU.mult)
         for u, s in enumerate(halves):
             nc.vector.scalar_tensor_tensor(focal[:, s], log_part[:, s], decay_sum[:], weight[:, s], ALU.add, ALU.mult,
                                            accum_out=focal_sum[:, u : u + 1])
@@ -173,18 +176,71 @@ def tile_attend_bfocal_heads_kernel(tc, hid, voc_words, voc_scales, mult, sw, ol
 
         norm = sb.tile([P, n], F32)
         nc.scalar.activation(norm[:], rescale[:], ACT.Identity, scale=neg_inv_z[:])
-        total_parts = sb.tile([P, 2], F32)
-        total = sb.tile([P, 1], F32)
-        nc.scalar.activation(total_parts[:], focal_sum[:], ACT.Identity, bias=sw_half_sum[:], accum_out=total[:])
+        early_sum = sb.tile([P, 1], F32)
+        nc.scalar.activation(early_sum[:], focal_sum[:, 0:1], ACT.Identity, bias=sw_sum[:])
+        early_coef = sb.tile([P, n], F32)
+        nc.scalar.activation(early_coef[:], norm[:], ACT.Identity, scale=early_sum[:])
         coef = sb.tile([P, n], F32)
-        nc.scalar.activation(coef[:], norm[:], ACT.Identity, scale=total[:])
+        for c in [1, 2, 3, 4, 0]:
+            nc.scalar.activation(coef[:, c : c + 1], focal_sum[:, 1:2], ACT.Identity, scale=norm[:, c : c + 1],
+                                 bias=early_coef[:, c : c + 1])
 
-        base = sb.tile([P, V], F32)
         result = sb.tile([P, V], F32)
-        for c in reversed(range(n)):
-            c0, width = CHUNKS[c]
-            cols = slice(c0, c0 + width)
-            nc.vector.scalar_tensor_tensor(base[:, cols], probs[:, cols], coef[:, c : c + 1], old_sb[:, cols],
-                                           ALU.mult, ALU.add)
-            nc.vector.tensor_tensor(result[:, cols], base[:, cols], placed[:, cols], ALU.add)
-            nc.sync.dma_start(out=out[:, cols], in_=result[:, cols])
+        scaled = sb.tile([P, V], F32)
+        turned = sb.tile([P, V], F32)
+        starts = list(range(PIECE, V, PIECE))
+        free_banks = [0, 1, 2, 3, 5, 6, 7]
+        tiles = range(PIECE // P)
+        turned_bank, back_bank = {}, {}
+
+        def chunk_of(c0):
+            return max(c for c in range(n) if CHUNKS[c][0] <= c0)
+
+        for k, c0 in enumerate(starts):
+            turned_bank[k] = ps.tile([P, PIECE], F32, name=f"turned{k}", tag=f"bank{free_banks[k]}")
+            for j in tiles:
+                nc.tensor.matmul(turned_bank[k][:, j * P : (j + 1) * P], old_sb[:, c0 + j * P : c0 + (j + 1) * P],
+                                 ident[:], start=(j == 0), stop=False, is_transpose=True)
+
+        def scale_and_turn(k):
+            c0 = starts[k]
+            c = chunk_of(c0)
+            nc.scalar.activation(scaled[:, c0 : c0 + PIECE], probs[:, c0 : c0 + PIECE], ACT.Copy,
+                                 scale=coef[:, c : c + 1])
+            for j in tiles:
+                nc.tensor.matmul(turned_bank[k][:, j * P : (j + 1) * P], scaled[:, c0 + j * P : c0 + (j + 1) * P],
+                                 ident[:], start=False, stop=(j == tiles[-1]), is_transpose=True)
+
+        def turn_back(k):
+            c0 = starts[k]
+            nc.scalar.copy(turned[:, c0 : c0 + PIECE], turned_bank[k][:])
+            back_bank[k] = ps.tile([P, PIECE], F32, name=f"back{k}", tag=f"bank{free_banks[k]}")
+            for j in tiles:
+                nc.tensor.transpose(back_bank[k][:, j * P : (j + 1) * P], turned[:, c0 + j * P : c0 + (j + 1) * P],
+                                    ident[:])
+
+        for step in range(len(starts) + LEAD):
+            if step < len(starts):
+                scale_and_turn(step)
+            if step >= LEAD:
+                turn_back(step - LEAD)
+
+        def add_placed(c0, summed):
+            nc.vector.tensor_tensor(result[:, c0 : c0 + PIECE], summed, placed[:, c0 : c0 + PIECE], ALU.add)
+
+        def store(c0, width):
+            nc.sync.dma_start(out=out[:, c0 : c0 + width], in_=result[:, c0 : c0 + width])
+
+        for k, c0 in enumerate(starts):
+            add_placed(c0, back_bank[k][:])
+            if k in (0, 5, 6):
+                store(c0, PIECE)
+            elif k in (2, 4):
+                store(c0 - PIECE, 2 * PIECE)
+            if k == 1:
+                base = turned[:, c0 : c0 + PIECE]
+                nc.vector.scalar_tensor_tensor(base, probs[:, :PIECE], coef[:, 0:1], old_sb[:, :PIECE],
+                                               ALU.mult, ALU.add)
+            if k == 2:
+                add_placed(0, base)
+                store(0, PIECE)

import math
from contextlib import ExitStack

import concourse.mybir as mybir
from concourse.masks import make_identity

D, V, Q, I = 512, 2048, 128, 512
FLOPS = 2 * D * Q * V

F32 = mybir.dt.float32
BF16 = mybir.dt.bfloat16
I32 = mybir.dt.int32
U32 = mybir.dt.uint32
U16 = mybir.dt.uint16
U8 = mybir.dt.uint8
FP8X4 = mybir.dt.float8_e4m3fn_x4
ALU = mybir.AluOpType
ACT = mybir.ActivationFunctionType
AXIS = mybir.AxisListType

P = 128
PACK = 4
BLOCK = 512
CHUNKS = [(0, 256), (256, 256), (512, 512), (1024, 512), (1536, 512)]
PAD = 8
PIECE = 256
LEAD = 3
LOAD = 512

NODE_STEP = 0.375
NODE_HI, NODE_LO = 9, -86
NODES = NODE_HI - NODE_LO + 1
NODE_CONST = NODE_STEP * sum(math.exp(-math.exp(NODE_STEP * j)) for j in range(NODE_LO, NODE_HI + 1))


def tile_attend_bfocal_heads_kernel(tc, hid, voc_words, voc_scales, mult, sw, old, offs, out):
    nc = tc.nc
    n = len(CHUNKS)
    with ExitStack() as ctx:
        sb = ctx.enter_context(tc.tile_pool(name="sb", bufs=1))
        ps = ctx.enter_context(tc.psum_pool(name="ps", bufs=1))

        planes = sb.tile([P, BLOCK], U8, align_bytes=64)
        nc.gpsimd.memset(planes[:].bitcast(I32), 0)

        hid_raw = sb.tile([P, PACK, Q], F32, tag="stage")
        nc.sync.dma_start(out=hid_raw[:], in_=hid.rearrange("(p t) q -> p t q", t=PACK))
        for quad in range(4):
            rows = voc_scales[0, 4 * quad : 4 * quad + 4, :].bitcast(I32)
            nc.sync.dma_start(
                out=planes[32 * quad : 32 * quad + 16, :].bitcast(I32),
                in_=rows.rearrange("r (b c) -> b r c", b=V // BLOCK),
            )
        words = []
        voc_bytes = voc_words[0].rearrange("p n t -> p (n t)")
        for b in range(V // LOAD):
            w = sb.tile([P, LOAD], U32, align_bytes=64, name=f"words{b}")
            nc.sync.dma_start(
                out=w[:].bitcast(I32),
                in_=voc_bytes[:, PACK * LOAD * b : PACK * LOAD * (b + 1)].bitcast(I32),
            )
            words.append(w)
        sw_cols = sb.tile([P, PACK], F32)
        nc.sync.dma_start(out=sw_cols[:], in_=sw.rearrange("o (p t) -> (o p) t", t=PACK))
        mult_col = sb.tile([P, 1], F32)
        nc.sync.dma_start(out=mult_col[:], in_=mult)
        offsets = sb.tile([P, I // 16], U16)
        nc.sync.dma_start(offsets[:], offs)

        placed = sb.tile([P, V], F32)
        nc.vector.memset(placed[:], 0.0)

        ident = sb.tile([P, P], F32)
        make_identity(nc, ident[:])
        steps = sb.tile([P, NODES], F32)
        nc.gpsimd.iota(steps[:], pattern=[[-1, NODES]], base=NODE_HI, channel_multiplier=0,
                       allow_small_or_imprecise_dtypes=True)
        nodes = sb.tile([P, NODES], F32)
        nc.scalar.activation(nodes[:], steps[:], ACT.Exp, scale=NODE_STEP)

        hid_bf = sb.tile([P, Q, PACK], BF16, align_bytes=64)
        hid_codes = sb.tile([P, Q], U32, align_bytes=64)
        hid_scales = sb.tile([P, Q], U8, align_bytes=64)
        half = Q // 2
        for u in range(2):
            qs = slice(u * half, (u + 1) * half)
            nc.vector.tensor_copy(
                out=hid_bf[:, qs, :].rearrange("p (c i) t -> p c t i", i=4),
                in_=hid_raw[:, :, qs].rearrange("p t (c i) -> p c t i", i=4),
            )
        old_sb = sb.tile([P, V], F32, tag="stage")
        nc.sync.dma_start(out=old_sb[:], in_=old)
        for u in range(2):
            qs = slice(u * half, (u + 1) * half)
            nc.vector.quantize_mx(
                out=hid_codes[:, qs].bitcast(FP8X4),
                scales=hid_scales[:, qs],
                in_=hid_bf[:, qs, :].rearrange("p q t -> p (q t)"),
            )

        scores = sb.tile([P, V], F32)
        probs = sb.tile([P, V], F32)
        chunk_max = sb.tile([P, n], F32)
        chunk_sum = sb.tile([P, n], F32)
        neg_ref = sb.tile([P, n, PAD], F32)
        neg_max = neg_ref[:, n - 1, 0:1]
        rescale = sb.tile([P, n], F32)
        shift = sb.tile([P, 1], F32)
        for c, (c0, width) in enumerate(CHUNKS):
            b, off = divmod(c0, BLOCK)
            bank = ps.tile([P, width], F32, name=f"score{c}", tag=f"bank{c}")
            nc.tensor.matmul_mx(
                out=bank[:],
                lhsT=hid_codes[:].bitcast(FP8X4),
                lhsT_scale=hid_scales[:],
                rhs=words[c0 // LOAD][:, c0 % LOAD : c0 % LOAD + width].bitcast(FP8X4),
                rhs_scale=planes[4 * b : P, off : off + width],
                start=True,
                stop=True,
            )
            cols = slice(c0, c0 + width)
            nc.vector.tensor_scalar(scores[:, cols], bank[:], 1.0, None, ALU.mult, ALU.max,
                                    accum_out=chunk_max[:, c : c + 1])
            if c < n - 1:
                nc.gpsimd.tensor_scalar(neg_ref[:, c, 0:1], chunk_max[:, c : c + 1], -1.0, 0.0, ALU.mult, ALU.add)
            else:
                nc.vector.tensor_reduce(neg_max, chunk_max[:], AXIS.X, ALU.max, negate=True)
                nc.scalar.activation(rescale[:], neg_ref[:, :, 0], ACT.Exp, scale=-1.0, bias=neg_max)
                nc.scalar.activation(shift[:], neg_max, ACT.Identity, bias=1.0 - NODE_CONST)
            nc.scalar.activation(probs[:, cols], scores[:, cols], ACT.Exp, bias=neg_ref[:, c, 0:1],
                                 accum_out=chunk_sum[:, c : c + 1])

        sw_bank = ps.tile([P, PACK, P], F32, tag=f"bank{n - 1}")
        for t in range(PACK):
            nc.tensor.transpose(sw_bank[:, t, :], sw_cols[:, t : t + 1].to_broadcast([P, P]), ident[:])
        row_scale = sb.tile([P, 1], F32)
        nc.gpsimd.tensor_scalar(row_scale[:], mult_col[:], 64.0 * NODE_STEP, 0.0, ALU.mult, ALU.add)
        sw_in_order = sw_bank[:].rearrange("p t s -> p s t")
        sw_mult = sb.tile([P, I], F32)
        nc.scalar.activation(sw_mult[:].rearrange("p (s t) -> p s t", t=PACK), sw_in_order, ACT.Copy,
                             scale=row_scale[:])

        picked = sb.tile([P, I], F32)
        nc.vector.tensor_copy(picked[:], scores[:].indirect(offsets[:]))

        terms = sb.tile([P, n], F32)
        neg_z = sb.tile([P, 1], F32)
        nc.vector.scalar_tensor_tensor(terms[:], rescale[:], -1.0, chunk_sum[:], ALU.mult, ALU.mult,
                                       accum_out=neg_z[:])
        halves = [slice(0, I // 2), slice(I // 2, I)]
        picked_p = sb.tile([P, I], F32)
        for s in halves:
            nc.scalar.activation(picked_p[:, s], picked[:, s], ACT.Exp, bias=neg_max)
        decay = sb.tile([P, NODES], F32, tag="stage2")
        decay_sum = sb.tile([P, 1], F32)
        nc.scalar.activation(decay[:], nodes[:], ACT.Exp, scale=neg_z[:], accum_out=decay_sum[:])
        sw64 = sb.tile([P, I], F32, tag="stage2")
        sw_sum = sb.tile([P, 1], F32)
        nc.scalar.activation(sw64[:].rearrange("p (s t) -> p s t", t=PACK), sw_in_order, ACT.Identity,
                             scale=64.0, accum_out=sw_sum[:])

        log_part = sb.tile([P, I], F32)
        nc.vector.tensor_scalar(log_part[:], picked[:], shift[:], 1.0 / NODE_STEP, ALU.add, ALU.mult)
        neg_inv_z = sb.tile([P, 1], F32)
        nc.vector.reciprocal(neg_inv_z[:], neg_z[:])
        weight = sb.tile([P, I], F32)
        focal = sb.tile([P, I], F32)
        focal_sum = sb.tile([P, 2], F32)
        for s in halves:
            nc.vector.scalar_tensor_tensor(weight[:, s], picked_p[:, s], neg_inv_z[:], sw_mult[:, s],
                                           ALU.mult, ALU.mult)
        for u, s in enumerate(halves):
            nc.vector.scalar_tensor_tensor(focal[:, s], log_part[:, s], decay_sum[:], weight[:, s], ALU.add, ALU.mult,
                                           accum_out=focal_sum[:, u : u + 1])
        nc.vector.tensor_tensor(placed[:].indirect(offsets[:]), focal[:], sw64[:], ALU.add)

        norm = sb.tile([P, n], F32)
        nc.scalar.activation(norm[:], rescale[:], ACT.Identity, scale=neg_inv_z[:])
        early_sum = sb.tile([P, 1], F32)
        nc.scalar.activation(early_sum[:], focal_sum[:, 0:1], ACT.Identity, bias=sw_sum[:])
        early_coef = sb.tile([P, n], F32)
        nc.scalar.activation(early_coef[:], norm[:], ACT.Identity, scale=early_sum[:])
        coef = sb.tile([P, n], F32)
        for c in [1, 2, 3, 4, 0]:
            nc.scalar.activation(coef[:, c : c + 1], focal_sum[:, 1:2], ACT.Identity, scale=norm[:, c : c + 1],
                                 bias=early_coef[:, c : c + 1])

        result = sb.tile([P, V], F32)
        scaled = sb.tile([P, V], F32)
        turned = sb.tile([P, V], F32)
        starts = list(range(PIECE, V, PIECE))
        free_banks = [0, 1, 2, 3, 5, 6, 7]
        tiles = range(PIECE // P)
        turned_bank, back_bank = {}, {}

        def chunk_of(c0):
            return max(c for c in range(n) if CHUNKS[c][0] <= c0)

        for k, c0 in enumerate(starts):
            turned_bank[k] = ps.tile([P, PIECE], F32, name=f"turned{k}", tag=f"bank{free_banks[k]}")
            for j in tiles:
                nc.tensor.matmul(turned_bank[k][:, j * P : (j + 1) * P], old_sb[:, c0 + j * P : c0 + (j + 1) * P],
                                 ident[:], start=(j == 0), stop=False, is_transpose=True)

        def scale_and_turn(k):
            c0 = starts[k]
            c = chunk_of(c0)
            nc.scalar.activation(scaled[:, c0 : c0 + PIECE], probs[:, c0 : c0 + PIECE], ACT.Copy,
                                 scale=coef[:, c : c + 1])
            for j in tiles:
                nc.tensor.matmul(turned_bank[k][:, j * P : (j + 1) * P], scaled[:, c0 + j * P : c0 + (j + 1) * P],
                                 ident[:], start=False, stop=(j == tiles[-1]), is_transpose=True)

        def turn_back(k):
            c0 = starts[k]
            nc.scalar.copy(turned[:, c0 : c0 + PIECE], turned_bank[k][:])
            back_bank[k] = ps.tile([P, PIECE], F32, name=f"back{k}", tag=f"bank{free_banks[k]}")
            for j in tiles:
                nc.tensor.transpose(back_bank[k][:, j * P : (j + 1) * P], turned[:, c0 + j * P : c0 + (j + 1) * P],
                                    ident[:])

        for step in range(len(starts) + LEAD):
            if step < len(starts):
                scale_and_turn(step)
            if step >= LEAD:
                turn_back(step - LEAD)

        def add_placed(c0, summed):
            nc.vector.tensor_tensor(result[:, c0 : c0 + PIECE], summed, placed[:, c0 : c0 + PIECE], ALU.add)

        def store(c0, width):
            nc.sync.dma_start(out=out[:, c0 : c0 + width], in_=result[:, c0 : c0 + width])

        for k, c0 in enumerate(starts):
            add_placed(c0, back_bank[k][:])
            if k in (0, 5, 6):
                store(c0, PIECE)
            elif k in (2, 4):
                store(c0 - PIECE, 2 * PIECE)
            if k == 1:
                base = turned[:, c0 : c0 + PIECE]
                nc.vector.scalar_tensor_tensor(base, probs[:, :PIECE], coef[:, 0:1], old_sb[:, :PIECE],
                                               ALU.mult, ALU.add)
            if k == 2:
                add_placed(0, base)
                store(0, PIECE)
